import numpy as np
import ml_dtypes

BF16 = ml_dtypes.bfloat16


def bf(x):
    return np.asarray(x, np.float32).astype(BF16)


def f32(x):
    return np.asarray(x, np.float32)


def f64(x):
    return np.asarray(x).astype(np.float64)


def striped(idx):
    return np.tile(idx.reshape(-1, 16).T, (8, 1))


S, K, M, N, E, Q = 256, 512, 128, 256, 4, 64


def gelu_tanh(v):
    return 0.5 * v * (1.0 + np.tanh(np.sqrt(2.0 / np.pi) * (v + 0.044715 * v**3)))


def setup_inputs():
    return {"base": bf(np.random.standard_normal((M, S))), "x": bf(np.random.standard_normal((K, N))), "w": bf(np.random.standard_normal((E, K, M)) / np.sqrt(K)), "b": f32(0.5 * np.random.standard_normal((M, 1))), "offs": striped(np.random.permutation(S))}


def reference(base, x, w, b, offs):
    idx = offs[:16].T.reshape(-1)
    z = f64(base).copy()
    for e in range(E):
        z[:, idx[e * Q : (e + 1) * Q]] += f64(w)[e].T @ f64(x)[:, e * Q : (e + 1) * Q]
    return gelu_tanh(z + f64(b))

@@ -1,0 +1,64 @@
+import concourse.mybir as mybir
+from concourse.masks import make_identity
+
+P = 128
+TOKENS = 256
+ENTRIES = 256
+EXPERTS = 4
+PIECE = ENTRIES // EXPERTS
+K_BLOCKS = 512 // P
+PER_COLUMN = 16
+
+FLOPS = 2 * 512 * P * ENTRIES
+
+BF16 = mybir.dt.bfloat16
+F32 = mybir.dt.float32
+U16 = mybir.dt.uint16
+
+
+def tile_scatter_matmul_kernel(tc, base, x, w, b, offs, out):
+    nc = tc.nc
+    with (
+        tc.tile_pool(name="held", bufs=1) as held,
+        tc.psum_pool(name="psum", bufs=1) as psum,
+    ):
+        offsets = held.tile([P, ENTRIES // PER_COLUMN], U16, name="offsets")
+        nc.sync.dma_start(offsets[:], offs)
+
+        base_tile = held.tile([P, TOKENS], BF16, name="base_tile")
+        nc.scalar.dma_start(base_tile[:], base)
+        bias = held.tile([P, 1], F32, name="bias")
+        nc.scalar.dma_start(bias[:], b)
+
+        x_tile = held.tile([P, K_BLOCKS, ENTRIES], BF16, name="x_tile")
+        nc.sync.dma_start(x_tile[:], x.rearrange("(p kb) j -> p kb j", kb=K_BLOCKS))
+        w_tiles = []
+        for e in range(EXPERTS):
+            w_tile = held.tile([P, K_BLOCKS, P], BF16, name="w_tile%d" % e)
+            queue = nc.sync if e % 2 == 0 else nc.scalar
+            queue.dma_start(w_tile[:], w[e].rearrange("(p kb) m -> p kb m", kb=K_BLOCKS))
+            w_tiles.append(w_tile)
+
+        identity = held.tile([P, P], BF16, name="identity")
+        make_identity(nc, identity[:])
+
+        window = psum.tile([P, TOKENS], F32, name="window")
+        nc.tensor.matmul(window[:], identity[:], base_tile[:], start=True, stop=False)
+
+        piece_columns = PIECE // PER_COLUMN
+        for e in range(EXPERTS):
+            piece = offsets[:, e * piece_columns : (e + 1) * piece_columns]
+            for kb in range(K_BLOCKS):
+                nc.tensor.matmul(
+                    window[:].indirect(piece),
+                    w_tiles[e][:, kb, :],
+                    x_tile[:, kb, e * PIECE : (e + 1) * PIECE],
+                    start=False,
+                    stop=(e == EXPERTS - 1 and kb == K_BLOCKS - 1),
+                )
+
+        result = held.tile([P, TOKENS], F32, name="result")
+        nc.scalar.activation(
+            result[:], window[:], mybir.ActivationFunctionType.Gelu_apprx_tanh, bias=bias[:]
+        )
+        nc.sync.dma_start(out, result[:])

@@ -8,12 +8,14 @@ EXPERTS = 4
 PIECE = ENTRIES // EXPERTS
 K_BLOCKS = 512 // P
 PER_COLUMN = 16
+WARM_TURNS = 16
 
 FLOPS = 2 * 512 * P * ENTRIES
 
 BF16 = mybir.dt.bfloat16
 F32 = mybir.dt.float32
 U16 = mybir.dt.uint16
+GELU = mybir.ActivationFunctionType.Gelu_apprx_tanh
 
 
 def tile_scatter_matmul_kernel(tc, base, x, w, b, offs, out):
@@ -24,20 +26,25 @@ def tile_scatter_matmul_kernel(tc, base, x, w, b, offs, out):
     ):
         offsets = held.tile([P, ENTRIES // PER_COLUMN], U16, name="offsets")
         nc.sync.dma_start(offsets[:], offs)
-
         base_tile = held.tile([P, TOKENS], BF16, name="base_tile")
-        nc.scalar.dma_start(base_tile[:], base)
-        bias = held.tile([P, 1], F32, name="bias")
-        nc.scalar.dma_start(bias[:], b)
-
+        nc.sync.dma_start(base_tile[:], base)
         x_tile = held.tile([P, K_BLOCKS, ENTRIES], BF16, name="x_tile")
         nc.sync.dma_start(x_tile[:], x.rearrange("(p kb) j -> p kb j", kb=K_BLOCKS))
         w_tiles = []
         for e in range(EXPERTS):
             w_tile = held.tile([P, K_BLOCKS, P], BF16, name="w_tile%d" % e)
-            queue = nc.sync if e % 2 == 0 else nc.scalar
-            queue.dma_start(w_tile[:], w[e].rearrange("(p kb) m -> p kb m", kb=K_BLOCKS))
+            nc.sync.dma_start(w_tile[:], w[e].rearrange("(p kb) m -> p kb m", kb=K_BLOCKS))
             w_tiles.append(w_tile)
+        bias = held.tile([P, 1], F32, name="bias")
+        nc.scalar.dma_start(bias[:], b)
+
+        zeros = held.tile([P, P], BF16, name="zeros")
+        nc.gpsimd.memset(zeros[:], 0.0)
+        unused = held.tile([P, 1], F32, name="unused")
+        nc.scalar.activation(unused[:], zeros[:, 0:1], GELU)
+        unread = psum.tile([P, P], F32, name="unread")
+        for turn in range(WARM_TURNS):
+            nc.tensor.matmul(unread[:], zeros[:], zeros[:], start=True, stop=True)
 
         identity = held.tile([P, P], BF16, name="identity")
         make_identity(nc, identity[:])
@@ -58,7 +65,5 @@ def tile_scatter_matmul_kernel(tc, base, x, w, b, offs, out):
                 )
 
         result = held.tile([P, TOKENS], F32, name="result")
-        nc.scalar.activation(
-            result[:], window[:], mybir.ActivationFunctionType.Gelu_apprx_tanh, bias=bias[:]
-        )
+        nc.scalar.activation(result[:], window[:], GELU, bias=bias[:])
         nc.sync.dma_start(out, result[:])

@@ -8,7 +8,6 @@ EXPERTS = 4
 PIECE = ENTRIES // EXPERTS
 K_BLOCKS = 512 // P
 PER_COLUMN = 16
-WARM_TURNS = 16
 
 FLOPS = 2 * 512 * P * ENTRIES
 
@@ -38,13 +37,10 @@ def tile_scatter_matmul_kernel(tc, base, x, w, b, offs, out):
         bias = held.tile([P, 1], F32, name="bias")
         nc.scalar.dma_start(bias[:], b)
 
-        zeros = held.tile([P, P], BF16, name="zeros")
+        zeros = held.tile([P, 1], BF16, name="zeros")
         nc.gpsimd.memset(zeros[:], 0.0)
         unused = held.tile([P, 1], F32, name="unused")
-        nc.scalar.activation(unused[:], zeros[:, 0:1], GELU)
-        unread = psum.tile([P, P], F32, name="unread")
-        for turn in range(WARM_TURNS):
-            nc.tensor.matmul(unread[:], zeros[:], zeros[:], start=True, stop=True)
+        nc.scalar.activation(unused[:], zeros[:], GELU)
 
         identity = held.tile([P, P], BF16, name="identity")
         make_identity(nc, identity[:])

@@ -7,7 +7,9 @@ ENTRIES = 256
 EXPERTS = 4
 PIECE = ENTRIES // EXPERTS
 K_BLOCKS = 512 // P
+HALF = K_BLOCKS // 2
 PER_COLUMN = 16
+WARM_TURNS = 16
 
 FLOPS = 2 * 512 * P * ENTRIES
 
@@ -27,20 +29,24 @@ def tile_scatter_matmul_kernel(tc, base, x, w, b, offs, out):
         nc.sync.dma_start(offsets[:], offs)
         base_tile = held.tile([P, TOKENS], BF16, name="base_tile")
         nc.sync.dma_start(base_tile[:], base)
-        x_tile = held.tile([P, K_BLOCKS, ENTRIES], BF16, name="x_tile")
-        nc.sync.dma_start(x_tile[:], x.rearrange("(p kb) j -> p kb j", kb=K_BLOCKS))
-        w_tiles = []
+        x_blocks = x.rearrange("(p kb) j -> p kb j", kb=K_BLOCKS)
+        x_halves = [held.tile([P, HALF, ENTRIES], BF16, name="x_half%d" % h) for h in range(2)]
+        w_tiles = [held.tile([P, K_BLOCKS, P], BF16, name="w_tile%d" % e) for e in range(EXPERTS)]
+        nc.sync.dma_start(x_halves[0][:], x_blocks[:, 0:HALF, :])
         for e in range(EXPERTS):
-            w_tile = held.tile([P, K_BLOCKS, P], BF16, name="w_tile%d" % e)
-            nc.sync.dma_start(w_tile[:], w[e].rearrange("(p kb) m -> p kb m", kb=K_BLOCKS))
-            w_tiles.append(w_tile)
+            nc.sync.dma_start(w_tiles[e][:], w[e].rearrange("(p kb) m -> p kb m", kb=K_BLOCKS))
+            if e == 0:
+                nc.sync.dma_start(x_halves[1][:], x_blocks[:, HALF:K_BLOCKS, :])
         bias = held.tile([P, 1], F32, name="bias")
         nc.scalar.dma_start(bias[:], b)
 
-        zeros = held.tile([P, 1], BF16, name="zeros")
+        zeros = held.tile([P, P], BF16, name="zeros")
         nc.gpsimd.memset(zeros[:], 0.0)
         unused = held.tile([P, 1], F32, name="unused")
-        nc.scalar.activation(unused[:], zeros[:], GELU)
+        nc.scalar.activation(unused[:], zeros[:, 0:1], GELU)
+        unread = psum.tile([P, P], F32, name="unread")
+        for turn in range(WARM_TURNS):
+            nc.tensor.matmul(unread[:], zeros[:], zeros[:], start=True, stop=True)
 
         identity = held.tile([P, P], BF16, name="identity")
         make_identity(nc, identity[:])
@@ -55,7 +61,7 @@ def tile_scatter_matmul_kernel(tc, base, x, w, b, offs, out):
                 nc.tensor.matmul(
                     window[:].indirect(piece),
                     w_tiles[e][:, kb, :],
-                    x_tile[:, kb, e * PIECE : (e + 1) * PIECE],
+                    x_halves[kb // HALF][:, kb % HALF, e * PIECE : (e + 1) * PIECE],
                     start=False,
                     stop=(e == EXPERTS - 1 and kb == K_BLOCKS - 1),
                 )

@@ -7,9 +7,8 @@ ENTRIES = 256
 EXPERTS = 4
 PIECE = ENTRIES // EXPERTS
 K_BLOCKS = 512 // P
-HALF = K_BLOCKS // 2
 PER_COLUMN = 16
-WARM_TURNS = 16
+WARM_TURNS = 12
 
 FLOPS = 2 * 512 * P * ENTRIES
 
@@ -26,19 +25,21 @@ def tile_scatter_matmul_kernel(tc, base, x, w, b, offs, out):
         tc.psum_pool(name="psum", bufs=1) as psum,
     ):
         offsets = held.tile([P, ENTRIES // PER_COLUMN], U16, name="offsets")
-        nc.sync.dma_start(offsets[:], offs)
         base_tile = held.tile([P, TOKENS], BF16, name="base_tile")
-        nc.sync.dma_start(base_tile[:], base)
-        x_blocks = x.rearrange("(p kb) j -> p kb j", kb=K_BLOCKS)
-        x_halves = [held.tile([P, HALF, ENTRIES], BF16, name="x_half%d" % h) for h in range(2)]
+        x_tile = held.tile([P, K_BLOCKS, ENTRIES], BF16, name="x_tile")
         w_tiles = [held.tile([P, K_BLOCKS, P], BF16, name="w_tile%d" % e) for e in range(EXPERTS)]
-        nc.sync.dma_start(x_halves[0][:], x_blocks[:, 0:HALF, :])
-        for e in range(EXPERTS):
-            nc.sync.dma_start(w_tiles[e][:], w[e].rearrange("(p kb) m -> p kb m", kb=K_BLOCKS))
-            if e == 0:
-                nc.sync.dma_start(x_halves[1][:], x_blocks[:, HALF:K_BLOCKS, :])
         bias = held.tile([P, 1], F32, name="bias")
-        nc.scalar.dma_start(bias[:], b)
+        x_blocks = x.rearrange("(p kb) j -> p kb j", kb=K_BLOCKS)
+        w_blocks = w.rearrange("e (p kb) m -> e p kb m", kb=K_BLOCKS)
+
+        nc.sync.dma_start(offsets[:], offs)
+        nc.scalar.dma_start(base_tile[:], base)
+        nc.sync.dma_start(x_tile[:], x_blocks)
+        nc.scalar.dma_start(w_tiles[0][:], w_blocks[0])
+        nc.scalar.dma_start(w_tiles[1][:], w_blocks[1])
+        nc.sync.dma_start(w_tiles[2][:], w_blocks[2])
+        nc.scalar.dma_start(w_tiles[3][:], w_blocks[3])
+        nc.sync.dma_start(bias[:], b)
 
         zeros = held.tile([P, P], BF16, name="zeros")
         nc.gpsimd.memset(zeros[:], 0.0)
@@ -61,7 +62,7 @@ def tile_scatter_matmul_kernel(tc, base, x, w, b, offs, out):
                 nc.tensor.matmul(
                     window[:].indirect(piece),
                     w_tiles[e][:, kb, :],
-                    x_halves[kb // HALF][:, kb % HALF, e * PIECE : (e + 1) * PIECE],
+                    x_tile[:, kb, e * PIECE : (e + 1) * PIECE],
                     start=False,
                     stop=(e == EXPERTS - 1 and kb == K_BLOCKS - 1),
                 )

@@ -7,6 +7,9 @@ ENTRIES = 256
 EXPERTS = 4
 PIECE = ENTRIES // EXPERTS
 K_BLOCKS = 512 // P
+HALVES = 2
+HALF_BLOCKS = K_BLOCKS // HALVES
+PAIR = 2
 PER_COLUMN = 16
 WARM_TURNS = 12
 
@@ -26,20 +29,25 @@ def tile_scatter_matmul_kernel(tc, base, x, w, b, offs, out):
     ):
         offsets = held.tile([P, ENTRIES // PER_COLUMN], U16, name="offsets")
         base_tile = held.tile([P, TOKENS], BF16, name="base_tile")
-        x_tile = held.tile([P, K_BLOCKS, ENTRIES], BF16, name="x_tile")
-        w_tiles = [held.tile([P, K_BLOCKS, P], BF16, name="w_tile%d" % e) for e in range(EXPERTS)]
+        x_halves = [held.tile([P, HALF_BLOCKS, ENTRIES], BF16, name="x_half%d" % h) for h in range(HALVES)]
+        w_parts = [
+            [held.tile([P, PAIR, HALF_BLOCKS, P], BF16, name="w_part%d_%d" % (h, g)) for g in range(EXPERTS // PAIR)]
+            for h in range(HALVES)
+        ]
         bias = held.tile([P, 1], F32, name="bias")
         x_blocks = x.rearrange("(p kb) j -> p kb j", kb=K_BLOCKS)
-        w_blocks = w.rearrange("e (p kb) m -> e p kb m", kb=K_BLOCKS)
+        w_blocks = w.rearrange("e (p kb) m -> p e kb m", kb=K_BLOCKS)
 
-        nc.sync.dma_start(offsets[:], offs)
-        nc.scalar.dma_start(base_tile[:], base)
-        nc.sync.dma_start(x_tile[:], x_blocks)
-        nc.scalar.dma_start(w_tiles[0][:], w_blocks[0])
-        nc.scalar.dma_start(w_tiles[1][:], w_blocks[1])
-        nc.sync.dma_start(w_tiles[2][:], w_blocks[2])
-        nc.scalar.dma_start(w_tiles[3][:], w_blocks[3])
-        nc.sync.dma_start(bias[:], b)
+        pieces = [(offsets[:], offs), (base_tile[:], base)]
+        for h in range(HALVES):
+            blocks = slice(h * HALF_BLOCKS, (h + 1) * HALF_BLOCKS)
+            pieces.append((x_halves[h][:], x_blocks[:, blocks, :]))
+            for g in range(EXPERTS // PAIR):
+                pieces.append((w_parts[h][g][:], w_blocks[:, g * PAIR : (g + 1) * PAIR, blocks, :]))
+        pieces.append((bias[:], b))
+        for turn, (tile_side, hbm_side) in enumerate(pieces):
+            queue = nc.sync if turn % 2 == 0 else nc.scalar
+            queue.dma_start(tile_side, hbm_side)
 
         zeros = held.tile([P, P], BF16, name="zeros")
         nc.gpsimd.memset(zeros[:], 0.0)
@@ -56,16 +64,17 @@ def tile_scatter_matmul_kernel(tc, base, x, w, b, offs, out):
         nc.tensor.matmul(window[:], identity[:], base_tile[:], start=True, stop=False)
 
         piece_columns = PIECE // PER_COLUMN
-        for e in range(EXPERTS):
-            piece = offsets[:, e * piece_columns : (e + 1) * piece_columns]
-            for kb in range(K_BLOCKS):
-                nc.tensor.matmul(
-                    window[:].indirect(piece),
-                    w_tiles[e][:, kb, :],
-                    x_tile[:, kb, e * PIECE : (e + 1) * PIECE],
-                    start=False,
-                    stop=(e == EXPERTS - 1 and kb == K_BLOCKS - 1),
-                )
+        for h in range(HALVES):
+            for e in range(EXPERTS):
+                piece = offsets[:, e * piece_columns : (e + 1) * piece_columns]
+                for kb in range(HALF_BLOCKS):
+                    nc.tensor.matmul(
+                        window[:].indirect(piece),
+                        w_parts[h][e // PAIR][:, e % PAIR, kb, :],
+                        x_halves[h][:, kb, e * PIECE : (e + 1) * PIECE],
+                        start=False,
+                        stop=(h == HALVES - 1 and e == EXPERTS - 1 and kb == HALF_BLOCKS - 1),
+                    )
 
         result = held.tile([P, TOKENS], F32, name="result")
         nc.scalar.activation(result[:], window[:], GELU, bias=bias[:])

@@ -9,7 +9,7 @@ PIECE = ENTRIES // EXPERTS
 K_BLOCKS = 512 // P
 HALVES = 2
 HALF_BLOCKS = K_BLOCKS // HALVES
-PAIR = 2
+SPLIT_EXPERTS = 2
 PER_COLUMN = 16
 WARM_TURNS = 12
 
@@ -30,21 +30,25 @@ def tile_scatter_matmul_kernel(tc, base, x, w, b, offs, out):
         offsets = held.tile([P, ENTRIES // PER_COLUMN], U16, name="offsets")
         base_tile = held.tile([P, TOKENS], BF16, name="base_tile")
         x_halves = [held.tile([P, HALF_BLOCKS, ENTRIES], BF16, name="x_half%d" % h) for h in range(HALVES)]
-        w_parts = [
-            [held.tile([P, PAIR, HALF_BLOCKS, P], BF16, name="w_part%d_%d" % (h, g)) for g in range(EXPERTS // PAIR)]
-            for h in range(HALVES)
-        ]
+        w_split = [held.tile([P, SPLIT_EXPERTS, HALF_BLOCKS, P], BF16, name="w_split%d" % h) for h in range(HALVES)]
+        w_whole = [held.tile([P, K_BLOCKS, P], BF16, name="w_whole%d" % e) for e in range(SPLIT_EXPERTS, EXPERTS)]
         bias = held.tile([P, 1], F32, name="bias")
         x_blocks = x.rearrange("(p kb) j -> p kb j", kb=K_BLOCKS)
         w_blocks = w.rearrange("e (p kb) m -> p e kb m", kb=K_BLOCKS)
 
-        pieces = [(offsets[:], offs), (base_tile[:], base)]
-        for h in range(HALVES):
-            blocks = slice(h * HALF_BLOCKS, (h + 1) * HALF_BLOCKS)
-            pieces.append((x_halves[h][:], x_blocks[:, blocks, :]))
-            for g in range(EXPERTS // PAIR):
-                pieces.append((w_parts[h][g][:], w_blocks[:, g * PAIR : (g + 1) * PAIR, blocks, :]))
-        pieces.append((bias[:], b))
+        first_half = slice(0, HALF_BLOCKS)
+        second_half = slice(HALF_BLOCKS, K_BLOCKS)
+        pieces = [
+            (offsets[:], offs),
+            (base_tile[:], base),
+            (x_halves[0][:], x_blocks[:, first_half, :]),
+            (w_split[0][:], w_blocks[:, 0:SPLIT_EXPERTS, first_half, :]),
+            (w_whole[0][:], w_blocks[:, SPLIT_EXPERTS, :, :]),
+            (w_whole[1][:], w_blocks[:, SPLIT_EXPERTS + 1, :, :]),
+            (x_halves[1][:], x_blocks[:, second_half, :]),
+            (w_split[1][:], w_blocks[:, 0:SPLIT_EXPERTS, second_half, :]),
+            (bias[:], b),
+        ]
         for turn, (tile_side, hbm_side) in enumerate(pieces):
             queue = nc.sync if turn % 2 == 0 else nc.scalar
             queue.dma_start(tile_side, hbm_side)
@@ -64,17 +68,22 @@ def tile_scatter_matmul_kernel(tc, base, x, w, b, offs, out):
         nc.tensor.matmul(window[:], identity[:], base_tile[:], start=True, stop=False)
 
         piece_columns = PIECE // PER_COLUMN
-        for h in range(HALVES):
-            for e in range(EXPERTS):
-                piece = offsets[:, e * piece_columns : (e + 1) * piece_columns]
-                for kb in range(HALF_BLOCKS):
-                    nc.tensor.matmul(
-                        window[:].indirect(piece),
-                        w_parts[h][e // PAIR][:, e % PAIR, kb, :],
-                        x_halves[h][:, kb, e * PIECE : (e + 1) * PIECE],
-                        start=False,
-                        stop=(h == HALVES - 1 and e == EXPERTS - 1 and kb == HALF_BLOCKS - 1),
-                    )
+        steps = [(0, e) for e in range(EXPERTS)]
+        steps += [(1, e) for e in range(SPLIT_EXPERTS, EXPERTS)] + [(1, e) for e in range(SPLIT_EXPERTS)]
+        for h, e in steps:
+            piece = offsets[:, e * piece_columns : (e + 1) * piece_columns]
+            for kb in range(HALF_BLOCKS):
+                if e < SPLIT_EXPERTS:
+                    weights = w_split[h][:, e, kb, :]
+                else:
+                    weights = w_whole[e - SPLIT_EXPERTS][:, h * HALF_BLOCKS + kb, :]
+                nc.tensor.matmul(
+                    window[:].indirect(piece),
+                    weights,
+                    x_halves[h][:, kb, e * PIECE : (e + 1) * PIECE],
+                    start=False,
+                    stop=((h, e) == steps[-1] and kb == HALF_BLOCKS - 1),
+                )
 
         result = held.tile([P, TOKENS], F32, name="result")
         nc.scalar.activation(result[:], window[:], GELU, bias=bias[:])

@@ -10,6 +10,7 @@ K_BLOCKS = 512 // P
 HALVES = 2
 HALF_BLOCKS = K_BLOCKS // HALVES
 SPLIT_EXPERTS = 2
+IN_FLIGHT = 8
 PER_COLUMN = 16
 WARM_TURNS = 12
 
@@ -30,7 +31,8 @@ def tile_scatter_matmul_kernel(tc, base, x, w, b, offs, out):
         offsets = held.tile([P, ENTRIES // PER_COLUMN], U16, name="offsets")
         base_tile = held.tile([P, TOKENS], BF16, name="base_tile")
         x_halves = [held.tile([P, HALF_BLOCKS, ENTRIES], BF16, name="x_half%d" % h) for h in range(HALVES)]
-        w_split = [held.tile([P, SPLIT_EXPERTS, HALF_BLOCKS, P], BF16, name="w_split%d" % h) for h in range(HALVES)]
+        w_first = [held.tile([P, HALF_BLOCKS, P], BF16, name="w_first%d" % e) for e in range(SPLIT_EXPERTS)]
+        w_second = held.tile([P, SPLIT_EXPERTS, HALF_BLOCKS, P], BF16, name="w_second")
         w_whole = [held.tile([P, K_BLOCKS, P], BF16, name="w_whole%d" % e) for e in range(SPLIT_EXPERTS, EXPERTS)]
         bias = held.tile([P, 1], F32, name="bias")
         x_blocks = x.rearrange("(p kb) j -> p kb j", kb=K_BLOCKS)
@@ -42,15 +44,16 @@ def tile_scatter_matmul_kernel(tc, base, x, w, b, offs, out):
             (offsets[:], offs),
             (base_tile[:], base),
             (x_halves[0][:], x_blocks[:, first_half, :]),
-            (w_split[0][:], w_blocks[:, 0:SPLIT_EXPERTS, first_half, :]),
+            (w_first[0][:], w_blocks[:, 0, first_half, :]),
+            (w_first[1][:], w_blocks[:, 1, first_half, :]),
             (w_whole[0][:], w_blocks[:, SPLIT_EXPERTS, :, :]),
             (w_whole[1][:], w_blocks[:, SPLIT_EXPERTS + 1, :, :]),
             (x_halves[1][:], x_blocks[:, second_half, :]),
-            (w_split[1][:], w_blocks[:, 0:SPLIT_EXPERTS, second_half, :]),
+            (w_second[:], w_blocks[:, 0:SPLIT_EXPERTS, second_half, :]),
             (bias[:], b),
         ]
         for turn, (tile_side, hbm_side) in enumerate(pieces):
-            queue = nc.sync if turn % 2 == 0 else nc.scalar
+            queue = nc.sync if turn % 2 == 0 or turn >= IN_FLIGHT else nc.scalar
             queue.dma_start(tile_side, hbm_side)
 
         zeros = held.tile([P, P], BF16, name="zeros")
@@ -73,8 +76,10 @@ def tile_scatter_matmul_kernel(tc, base, x, w, b, offs, out):
         for h, e in steps:
             piece = offsets[:, e * piece_columns : (e + 1) * piece_columns]
             for kb in range(HALF_BLOCKS):
-                if e < SPLIT_EXPERTS:
-                    weights = w_split[h][:, e, kb, :]
+                if e < SPLIT_EXPERTS and h == 0:
+                    weights = w_first[e][:, kb, :]
+                elif e < SPLIT_EXPERTS:
+                    weights = w_second[:, e, kb, :]
                 else:
                     weights = w_whole[e - SPLIT_EXPERTS][:, h * HALF_BLOCKS + kb, :]
                 nc.tensor.matmul(

@@ -10,7 +10,6 @@ K_BLOCKS = 512 // P
 HALVES = 2
 HALF_BLOCKS = K_BLOCKS // HALVES
 SPLIT_EXPERTS = 2
-IN_FLIGHT = 8
 PER_COLUMN = 16
 WARM_TURNS = 12
 
@@ -53,7 +52,7 @@ def tile_scatter_matmul_kernel(tc, base, x, w, b, offs, out):
             (bias[:], b),
         ]
         for turn, (tile_side, hbm_side) in enumerate(pieces):
-            queue = nc.sync if turn % 2 == 0 or turn >= IN_FLIGHT else nc.scalar
+            queue = nc.sync if turn % 2 == 0 else nc.scalar
             queue.dma_start(tile_side, hbm_side)
 
         zeros = held.tile([P, P], BF16, name="zeros")

@@ -12,6 +12,7 @@ HALF_BLOCKS = K_BLOCKS // HALVES
 SPLIT_EXPERTS = 2
 PER_COLUMN = 16
 WARM_TURNS = 12
+BLOCK = 32
 
 FLOPS = 2 * 512 * P * ENTRIES
 
@@ -33,7 +34,9 @@ def tile_scatter_matmul_kernel(tc, base, x, w, b, offs, out):
         w_first = [held.tile([P, HALF_BLOCKS, P], BF16, name="w_first%d" % e) for e in range(SPLIT_EXPERTS)]
         w_second = held.tile([P, SPLIT_EXPERTS, HALF_BLOCKS, P], BF16, name="w_second")
         w_whole = [held.tile([P, K_BLOCKS, P], BF16, name="w_whole%d" % e) for e in range(SPLIT_EXPERTS, EXPERTS)]
-        bias = held.tile([P, 1], F32, name="bias")
+        bias_rows = held.tile([P, BLOCK], F32, name="bias_rows", align_bytes=64)
+        bias_columns = held.tile([P, BLOCK], F32, name="bias_columns", align_bytes=64)
+        nc.vector.memset(bias_rows[:], 0.0)
         x_blocks = x.rearrange("(p kb) j -> p kb j", kb=K_BLOCKS)
         w_blocks = w.rearrange("e (p kb) m -> p e kb m", kb=K_BLOCKS)
 
@@ -49,11 +52,13 @@ def tile_scatter_matmul_kernel(tc, base, x, w, b, offs, out):
             (w_whole[1][:], w_blocks[:, SPLIT_EXPERTS + 1, :, :]),
             (x_halves[1][:], x_blocks[:, second_half, :]),
             (w_second[:], w_blocks[:, 0:SPLIT_EXPERTS, second_half, :]),
-            (bias[:], b),
+            (bias_rows[0:P:BLOCK, :], b.rearrange("(q i) o -> q (i o)", i=BLOCK)),
         ]
         for turn, (tile_side, hbm_side) in enumerate(pieces):
             queue = nc.sync if turn % 2 == 0 else nc.scalar
             queue.dma_start(tile_side, hbm_side)
+
+        nc.vector.transpose(bias_columns[:], bias_rows[:])
 
         zeros = held.tile([P, P], BF16, name="zeros")
         nc.gpsimd.memset(zeros[:], 0.0)
@@ -90,5 +95,5 @@ def tile_scatter_matmul_kernel(tc, base, x, w, b, offs, out):
                 )
 
         result = held.tile([P, TOKENS], F32, name="result")
-        nc.scalar.activation(result[:], window[:], GELU, bias=bias[:])
+        nc.scalar.activation(result[:], window[:], GELU, bias=bias_columns[:, 0:1])
         nc.sync.dma_start(out, result[:])

@@ -11,7 +11,7 @@ HALVES = 2
 HALF_BLOCKS = K_BLOCKS // HALVES
 SPLIT_EXPERTS = 2
 PER_COLUMN = 16
-WARM_TURNS = 12
+WARM_TURNS = 10
 BLOCK = 32
 
 FLOPS = 2 * 512 * P * ENTRIES

@@ -9,7 +9,6 @@ PIECE = ENTRIES // EXPERTS
 K_BLOCKS = 512 // P
 HALVES = 2
 HALF_BLOCKS = K_BLOCKS // HALVES
-SPLIT_EXPERTS = 2
 PER_COLUMN = 16
 WARM_TURNS = 10
 BLOCK = 32
@@ -31,9 +30,8 @@ def tile_scatter_matmul_kernel(tc, base, x, w, b, offs, out):
         offsets = held.tile([P, ENTRIES // PER_COLUMN], U16, name="offsets")
         base_tile = held.tile([P, TOKENS], BF16, name="base_tile")
         x_halves = [held.tile([P, HALF_BLOCKS, ENTRIES], BF16, name="x_half%d" % h) for h in range(HALVES)]
-        w_first = [held.tile([P, HALF_BLOCKS, P], BF16, name="w_first%d" % e) for e in range(SPLIT_EXPERTS)]
-        w_second = held.tile([P, SPLIT_EXPERTS, HALF_BLOCKS, P], BF16, name="w_second")
-        w_whole = [held.tile([P, K_BLOCKS, P], BF16, name="w_whole%d" % e) for e in range(SPLIT_EXPERTS, EXPERTS)]
+        w_cut = [held.tile([P, HALF_BLOCKS, P], BF16, name="w_cut%d" % h) for h in range(HALVES)]
+        w_whole = [held.tile([P, K_BLOCKS, P], BF16, name="w_whole%d" % e) for e in range(1, EXPERTS)]
         bias_rows = held.tile([P, BLOCK], F32, name="bias_rows", align_bytes=64)
         bias_columns = held.tile([P, BLOCK], F32, name="bias_columns", align_bytes=64)
         nc.vector.memset(bias_rows[:], 0.0)
@@ -46,12 +44,12 @@ def tile_scatter_matmul_kernel(tc, base, x, w, b, offs, out):
             (offsets[:], offs),
             (base_tile[:], base),
             (x_halves[0][:], x_blocks[:, first_half, :]),
-            (w_first[0][:], w_blocks[:, 0, first_half, :]),
-            (w_first[1][:], w_blocks[:, 1, first_half, :]),
-            (w_whole[0][:], w_blocks[:, SPLIT_EXPERTS, :, :]),
-            (w_whole[1][:], w_blocks[:, SPLIT_EXPERTS + 1, :, :]),
+            (w_cut[0][:], w_blocks[:, 0, first_half, :]),
+            (w_whole[0][:], w_blocks[:, 1, :, :]),
             (x_halves[1][:], x_blocks[:, second_half, :]),
-            (w_second[:], w_blocks[:, 0:SPLIT_EXPERTS, second_half, :]),
+            (w_whole[1][:], w_blocks[:, 2, :, :]),
+            (w_whole[2][:], w_blocks[:, 3, :, :]),
+            (w_cut[1][:], w_blocks[:, 0, second_half, :]),
             (bias_rows[0:P:BLOCK, :], b.rearrange("(q i) o -> q (i o)", i=BLOCK)),
         ]
         for turn, (tile_side, hbm_side) in enumerate(pieces):
@@ -75,17 +73,14 @@ def tile_scatter_matmul_kernel(tc, base, x, w, b, offs, out):
         nc.tensor.matmul(window[:], identity[:], base_tile[:], start=True, stop=False)
 
         piece_columns = PIECE // PER_COLUMN
-        steps = [(0, e) for e in range(EXPERTS)]
-        steps += [(1, e) for e in range(SPLIT_EXPERTS, EXPERTS)] + [(1, e) for e in range(SPLIT_EXPERTS)]
+        steps = [(0, 0)] + [(h, e) for e in range(1, EXPERTS) for h in range(HALVES)] + [(1, 0)]
         for h, e in steps:
             piece = offsets[:, e * piece_columns : (e + 1) * piece_columns]
             for kb in range(HALF_BLOCKS):
-                if e < SPLIT_EXPERTS and h == 0:
-                    weights = w_first[e][:, kb, :]
-                elif e < SPLIT_EXPERTS:
-                    weights = w_second[:, e, kb, :]
+                if e == 0:
+                    weights = w_cut[h][:, kb, :]
                 else:
-                    weights = w_whole[e - SPLIT_EXPERTS][:, h * HALF_BLOCKS + kb, :]
+                    weights = w_whole[e - 1][:, h * HALF_BLOCKS + kb, :]
                 nc.tensor.matmul(
                     window[:].indirect(piece),
                     weights,

@@ -12,6 +12,7 @@ HALF_BLOCKS = K_BLOCKS // HALVES
 PER_COLUMN = 16
 WARM_TURNS = 10
 BLOCK = 32
+BURST = 256
 
 FLOPS = 2 * 512 * P * ENTRIES
 
@@ -28,10 +29,10 @@ def tile_scatter_matmul_kernel(tc, base, x, w, b, offs, out):
         tc.psum_pool(name="psum", bufs=1) as psum,
     ):
         offsets = held.tile([P, ENTRIES // PER_COLUMN], U16, name="offsets")
-        base_tile = held.tile([P, TOKENS], BF16, name="base_tile")
-        x_halves = [held.tile([P, HALF_BLOCKS, ENTRIES], BF16, name="x_half%d" % h) for h in range(HALVES)]
-        w_cut = [held.tile([P, HALF_BLOCKS, P], BF16, name="w_cut%d" % h) for h in range(HALVES)]
-        w_whole = [held.tile([P, K_BLOCKS, P], BF16, name="w_whole%d" % e) for e in range(1, EXPERTS)]
+        base_tile = held.tile([P, TOKENS], BF16, name="base_tile", align_bytes=BURST)
+        x_halves = [held.tile([P, HALF_BLOCKS, ENTRIES], BF16, name="x_half%d" % h, align_bytes=BURST) for h in range(HALVES)]
+        w_cut = [held.tile([P, HALF_BLOCKS, P], BF16, name="w_cut%d" % h, align_bytes=BURST) for h in range(HALVES)]
+        w_whole = [held.tile([P, K_BLOCKS, P], BF16, name="w_whole%d" % e, align_bytes=BURST) for e in range(1, EXPERTS)]
         bias_rows = held.tile([P, BLOCK], F32, name="bias_rows", align_bytes=64)
         bias_columns = held.tile([P, BLOCK], F32, name="bias_columns", align_bytes=64)
         nc.vector.memset(bias_rows[:], 0.0)
@@ -89,6 +90,6 @@ def tile_scatter_matmul_kernel(tc, base, x, w, b, offs, out):
                     stop=((h, e) == steps[-1] and kb == HALF_BLOCKS - 1),
                 )
 
-        result = held.tile([P, TOKENS], F32, name="result")
+        result = held.tile([P, TOKENS], F32, name="result", align_bytes=BURST)
         nc.scalar.activation(result[:], window[:], GELU, bias=bias_columns[:, 0:1])
         nc.sync.dma_start(out, result[:])

@@ -59,13 +59,14 @@ def tile_scatter_matmul_kernel(tc, base, x, w, b, offs, out):
 
         nc.vector.transpose(bias_columns[:], bias_rows[:])
 
-        zeros = held.tile([P, P], BF16, name="zeros")
+        zeros = held.tile([P, PER_COLUMN], BF16, name="zeros")
         nc.gpsimd.memset(zeros[:], 0.0)
         unused = held.tile([P, 1], F32, name="unused")
         nc.scalar.activation(unused[:], zeros[:, 0:1], GELU)
         unread = psum.tile([P, P], F32, name="unread")
+        zero_block = zeros[:, 0:1].to_broadcast([P, P])
         for turn in range(WARM_TURNS):
-            nc.tensor.matmul(unread[:], zeros[:], zeros[:], start=True, stop=True)
+            nc.tensor.matmul(unread[:], zero_block, zero_block, start=True, stop=True)
 
         identity = held.tile([P, P], BF16, name="identity")
         make_identity(nc, identity[:])

@@ -12,7 +12,7 @@ HALF_BLOCKS = K_BLOCKS // HALVES
 PER_COLUMN = 16
 WARM_TURNS = 10
 BLOCK = 32
-BURST = 256
+BURST = 1024
 
 FLOPS = 2 * 512 * P * ENTRIES
 

@@ -9,6 +9,7 @@ PIECE = ENTRIES // EXPERTS
 K_BLOCKS = 512 // P
 HALVES = 2
 HALF_BLOCKS = K_BLOCKS // HALVES
+CUT_EXPERTS = 2
 PER_COLUMN = 16
 WARM_TURNS = 10
 BLOCK = 32
@@ -31,8 +32,9 @@ def tile_scatter_matmul_kernel(tc, base, x, w, b, offs, out):
         offsets = held.tile([P, ENTRIES // PER_COLUMN], U16, name="offsets")
         base_tile = held.tile([P, TOKENS], BF16, name="base_tile", align_bytes=BURST)
         x_halves = [held.tile([P, HALF_BLOCKS, ENTRIES], BF16, name="x_half%d" % h, align_bytes=BURST) for h in range(HALVES)]
-        w_cut = [held.tile([P, HALF_BLOCKS, P], BF16, name="w_cut%d" % h, align_bytes=BURST) for h in range(HALVES)]
-        w_whole = [held.tile([P, K_BLOCKS, P], BF16, name="w_whole%d" % e, align_bytes=BURST) for e in range(1, EXPERTS)]
+        w_first = [held.tile([P, HALF_BLOCKS, P], BF16, name="w_first%d" % e, align_bytes=BURST) for e in range(CUT_EXPERTS)]
+        w_second = held.tile([P, CUT_EXPERTS, HALF_BLOCKS, P], BF16, name="w_second", align_bytes=BURST)
+        w_whole = [held.tile([P, K_BLOCKS, P], BF16, name="w_whole%d" % e, align_bytes=BURST) for e in range(CUT_EXPERTS, EXPERTS)]
         bias_rows = held.tile([P, BLOCK], F32, name="bias_rows", align_bytes=64)
         bias_columns = held.tile([P, BLOCK], F32, name="bias_columns", align_bytes=64)
         nc.vector.memset(bias_rows[:], 0.0)
@@ -45,12 +47,12 @@ def tile_scatter_matmul_kernel(tc, base, x, w, b, offs, out):
             (offsets[:], offs),
             (base_tile[:], base),
             (x_halves[0][:], x_blocks[:, first_half, :]),
-            (w_cut[0][:], w_blocks[:, 0, first_half, :]),
-            (w_whole[0][:], w_blocks[:, 1, :, :]),
+            (w_first[0][:], w_blocks[:, 0, first_half, :]),
+            (w_first[1][:], w_blocks[:, 1, first_half, :]),
+            (w_whole[0][:], w_blocks[:, 2, :, :]),
             (x_halves[1][:], x_blocks[:, second_half, :]),
-            (w_whole[1][:], w_blocks[:, 2, :, :]),
-            (w_whole[2][:], w_blocks[:, 3, :, :]),
-            (w_cut[1][:], w_blocks[:, 0, second_half, :]),
+            (w_whole[1][:], w_blocks[:, 3, :, :]),
+            (w_second[:], w_blocks[:, 0:CUT_EXPERTS, second_half, :]),
             (bias_rows[0:P:BLOCK, :], b.rearrange("(q i) o -> q (i o)", i=BLOCK)),
         ]
         for turn, (tile_side, hbm_side) in enumerate(pieces):
@@ -75,14 +77,20 @@ def tile_scatter_matmul_kernel(tc, base, x, w, b, offs, out):
         nc.tensor.matmul(window[:], identity[:], base_tile[:], start=True, stop=False)
 
         piece_columns = PIECE // PER_COLUMN
-        steps = [(0, 0)] + [(h, e) for e in range(1, EXPERTS) for h in range(HALVES)] + [(1, 0)]
+        steps = (
+            [(0, e) for e in range(CUT_EXPERTS)]
+            + [(h, e) for e in range(CUT_EXPERTS, EXPERTS) for h in range(HALVES)]
+            + [(1, e) for e in range(CUT_EXPERTS)]
+        )
         for h, e in steps:
             piece = offsets[:, e * piece_columns : (e + 1) * piece_columns]
             for kb in range(HALF_BLOCKS):
-                if e == 0:
-                    weights = w_cut[h][:, kb, :]
+                if e >= CUT_EXPERTS:
+                    weights = w_whole[e - CUT_EXPERTS][:, h * HALF_BLOCKS + kb, :]
+                elif h == 0:
+                    weights = w_first[e][:, kb, :]
                 else:
-                    weights = w_whole[e - 1][:, h * HALF_BLOCKS + kb, :]
+                    weights = w_second[:, e, kb, :]
                 nc.tensor.matmul(
                     window[:].indirect(piece),
                     weights,

@@ -50,8 +50,8 @@ def tile_scatter_matmul_kernel(tc, base, x, w, b, offs, out):
             (w_first[0][:], w_blocks[:, 0, first_half, :]),
             (w_first[1][:], w_blocks[:, 1, first_half, :]),
             (w_whole[0][:], w_blocks[:, 2, :, :]),
-            (x_halves[1][:], x_blocks[:, second_half, :]),
             (w_whole[1][:], w_blocks[:, 3, :, :]),
+            (x_halves[1][:], x_blocks[:, second_half, :]),
             (w_second[:], w_blocks[:, 0:CUT_EXPERTS, second_half, :]),
             (bias_rows[0:P:BLOCK, :], b.rearrange("(q i) o -> q (i o)", i=BLOCK)),
         ]
@@ -77,27 +77,25 @@ def tile_scatter_matmul_kernel(tc, base, x, w, b, offs, out):
         nc.tensor.matmul(window[:], identity[:], base_tile[:], start=True, stop=False)
 
         piece_columns = PIECE // PER_COLUMN
-        steps = (
-            [(0, e) for e in range(CUT_EXPERTS)]
-            + [(h, e) for e in range(CUT_EXPERTS, EXPERTS) for h in range(HALVES)]
-            + [(1, e) for e in range(CUT_EXPERTS)]
-        )
-        for h, e in steps:
-            piece = offsets[:, e * piece_columns : (e + 1) * piece_columns]
+        cut_pair = list(range(CUT_EXPERTS))
+        whole_pair = list(range(CUT_EXPERTS, EXPERTS))
+        steps = [(0, cut_pair), (0, whole_pair), (1, whole_pair), (1, cut_pair)]
+        for h, pair in steps:
             for kb in range(HALF_BLOCKS):
-                if e >= CUT_EXPERTS:
-                    weights = w_whole[e - CUT_EXPERTS][:, h * HALF_BLOCKS + kb, :]
-                elif h == 0:
-                    weights = w_first[e][:, kb, :]
-                else:
-                    weights = w_second[:, e, kb, :]
-                nc.tensor.matmul(
-                    window[:].indirect(piece),
-                    weights,
-                    x_halves[h][:, kb, e * PIECE : (e + 1) * PIECE],
-                    start=False,
-                    stop=((h, e) == steps[-1] and kb == HALF_BLOCKS - 1),
-                )
+                for e in pair:
+                    if e >= CUT_EXPERTS:
+                        weights = w_whole[e - CUT_EXPERTS][:, h * HALF_BLOCKS + kb, :]
+                    elif h == 0:
+                        weights = w_first[e][:, kb, :]
+                    else:
+                        weights = w_second[:, e, kb, :]
+                    nc.tensor.matmul(
+                        window[:].indirect(offsets[:, e * piece_columns : (e + 1) * piece_columns]),
+                        weights,
+                        x_halves[h][:, kb, e * PIECE : (e + 1) * PIECE],
+                        start=False,
+                        stop=((h, pair) == steps[-1] and kb == HALF_BLOCKS - 1 and e == pair[-1]),
+                    )
 
         result = held.tile([P, TOKENS], F32, name="result", align_bytes=BURST)
         nc.scalar.activation(result[:], window[:], GELU, bias=bias_columns[:, 0:1])

@@ -46,8 +46,8 @@ def tile_scatter_matmul_kernel(tc, base, x, w, b, offs, out):
         pieces = [
             (offsets[:], offs),
             (base_tile[:], base),
-            (x_halves[0][:], x_blocks[:, first_half, :]),
             (w_first[0][:], w_blocks[:, 0, first_half, :]),
+            (x_halves[0][:], x_blocks[:, first_half, :]),
             (w_first[1][:], w_blocks[:, 1, first_half, :]),
             (w_whole[0][:], w_blocks[:, 2, :, :]),
             (w_whole[1][:], w_blocks[:, 3, :, :]),

@@ -30,6 +30,8 @@ def tile_scatter_matmul_kernel(tc, base, x, w, b, offs, out):
         tc.psum_pool(name="psum", bufs=1) as psum,
     ):
         offsets = held.tile([P, ENTRIES // PER_COLUMN], U16, name="offsets")
+        zeros = held.tile([P, PER_COLUMN], BF16, name="zeros")
+        nc.vector.memset(zeros[:], 0.0)
         base_tile = held.tile([P, TOKENS], BF16, name="base_tile", align_bytes=BURST)
         x_halves = [held.tile([P, HALF_BLOCKS, ENTRIES], BF16, name="x_half%d" % h, align_bytes=BURST) for h in range(HALVES)]
         w_first = [held.tile([P, HALF_BLOCKS, P], BF16, name="w_first%d" % e, align_bytes=BURST) for e in range(CUT_EXPERTS)]
@@ -61,8 +63,6 @@ def tile_scatter_matmul_kernel(tc, base, x, w, b, offs, out):
 
         nc.vector.transpose(bias_columns[:], bias_rows[:])
 
-        zeros = held.tile([P, PER_COLUMN], BF16, name="zeros")
-        nc.gpsimd.memset(zeros[:], 0.0)
         unused = held.tile([P, 1], F32, name="unused")
         nc.scalar.activation(unused[:], zeros[:, 0:1], GELU)
         unread = psum.tile([P, P], F32, name="unread")

@@ -1,5 +1,4 @@
 import concourse.mybir as mybir
-from concourse.masks import make_identity
 
 P = 128
 TOKENS = 256
@@ -21,6 +20,7 @@ BF16 = mybir.dt.bfloat16
 F32 = mybir.dt.float32
 U16 = mybir.dt.uint16
 GELU = mybir.ActivationFunctionType.Gelu_apprx_tanh
+ALU = mybir.AluOpType
 
 
 def tile_scatter_matmul_kernel(tc, base, x, w, b, offs, out):
@@ -61,8 +61,6 @@ def tile_scatter_matmul_kernel(tc, base, x, w, b, offs, out):
             queue = nc.sync if turn % 2 == 0 else nc.scalar
             queue.dma_start(tile_side, hbm_side)
 
-        nc.vector.transpose(bias_columns[:], bias_rows[:])
-
         unused = held.tile([P, 1], F32, name="unused")
         nc.scalar.activation(unused[:], zeros[:, 0:1], GELU)
         unread = psum.tile([P, P], F32, name="unread")
@@ -70,8 +68,24 @@ def tile_scatter_matmul_kernel(tc, base, x, w, b, offs, out):
         for turn in range(WARM_TURNS):
             nc.tensor.matmul(unread[:], zero_block, zero_block, start=True, stop=True)
 
+        ones = held.tile([P, BLOCK], F32, name="ones", align_bytes=64)
+        column_number = held.tile([P, BLOCK], F32, name="column_number", align_bytes=64)
+        row_number = held.tile([P, BLOCK], F32, name="row_number", align_bytes=64)
         identity = held.tile([P, P], BF16, name="identity")
-        make_identity(nc, identity[:])
+        nc.vector.memset(ones[:], 1.0)
+        nc.vector.tensor_tensor_scan(column_number[:], ones[:], ones[:], 0.0, ALU.mult, ALU.add)
+        nc.vector.transpose(row_number[:], column_number[:])
+        nc.vector.memset(identity[:], 0.0)
+        for q in range(P // BLOCK):
+            rows = slice(q * BLOCK, (q + 1) * BLOCK)
+            nc.vector.tensor_scalar(
+                out=identity[rows, rows],
+                in0=column_number[rows, :],
+                scalar1=row_number[rows, 0:1],
+                scalar2=None,
+                op0=ALU.is_equal,
+            )
+        nc.vector.transpose(bias_columns[:], bias_rows[:])
 
         window = psum.tile([P, TOKENS], F32, name="window")
         nc.tensor.matmul(window[:], identity[:], base_tile[:], start=True, stop=False)

import concourse.mybir as mybir

P = 128
TOKENS = 256
ENTRIES = 256
EXPERTS = 4
PIECE = ENTRIES // EXPERTS
K_BLOCKS = 512 // P
HALVES = 2
HALF_BLOCKS = K_BLOCKS // HALVES
CUT_EXPERTS = 2
PER_COLUMN = 16
WARM_TURNS = 10
BLOCK = 32
BURST = 1024

FLOPS = 2 * 512 * P * ENTRIES

BF16 = mybir.dt.bfloat16
F32 = mybir.dt.float32
U16 = mybir.dt.uint16
GELU = mybir.ActivationFunctionType.Gelu_apprx_tanh
ALU = mybir.AluOpType


def tile_scatter_matmul_kernel(tc, base, x, w, b, offs, out):
    nc = tc.nc
    with (
        tc.tile_pool(name="held", bufs=1) as held,
        tc.psum_pool(name="psum", bufs=1) as psum,
    ):
        offsets = held.tile([P, ENTRIES // PER_COLUMN], U16, name="offsets")
        zeros = held.tile([P, PER_COLUMN], BF16, name="zeros")
        nc.vector.memset(zeros[:], 0.0)
        base_tile = held.tile([P, TOKENS], BF16, name="base_tile", align_bytes=BURST)
        x_halves = [held.tile([P, HALF_BLOCKS, ENTRIES], BF16, name="x_half%d" % h, align_bytes=BURST) for h in range(HALVES)]
        w_first = [held.tile([P, HALF_BLOCKS, P], BF16, name="w_first%d" % e, align_bytes=BURST) for e in range(CUT_EXPERTS)]
        w_second = held.tile([P, CUT_EXPERTS, HALF_BLOCKS, P], BF16, name="w_second", align_bytes=BURST)
        w_whole = [held.tile([P, K_BLOCKS, P], BF16, name="w_whole%d" % e, align_bytes=BURST) for e in range(CUT_EXPERTS, EXPERTS)]
        bias_rows = held.tile([P, BLOCK], F32, name="bias_rows", align_bytes=64)
        bias_columns = held.tile([P, BLOCK], F32, name="bias_columns", align_bytes=64)
        nc.vector.memset(bias_rows[:], 0.0)
        x_blocks = x.rearrange("(p kb) j -> p kb j", kb=K_BLOCKS)
        w_blocks = w.rearrange("e (p kb) m -> p e kb m", kb=K_BLOCKS)

        first_half = slice(0, HALF_BLOCKS)
        second_half = slice(HALF_BLOCKS, K_BLOCKS)
        pieces = [
            (offsets[:], offs),
            (base_tile[:], base),
            (w_first[0][:], w_blocks[:, 0, first_half, :]),
            (x_halves[0][:], x_blocks[:, first_half, :]),
            (w_first[1][:], w_blocks[:, 1, first_half, :]),
            (w_whole[0][:], w_blocks[:, 2, :, :]),
            (w_whole[1][:], w_blocks[:, 3, :, :]),
            (x_halves[1][:], x_blocks[:, second_half, :]),
            (w_second[:], w_blocks[:, 0:CUT_EXPERTS, second_half, :]),
            (bias_rows[0:P:BLOCK, :], b.rearrange("(q i) o -> q (i o)", i=BLOCK)),
        ]
        for turn, (tile_side, hbm_side) in enumerate(pieces):
            queue = nc.sync if turn % 2 == 0 else nc.scalar
            queue.dma_start(tile_side, hbm_side)

        unused = held.tile([P, 1], F32, name="unused")
        nc.scalar.activation(unused[:], zeros[:, 0:1], GELU)
        unread = psum.tile([P, P], F32, name="unread")
        zero_block = zeros[:, 0:1].to_broadcast([P, P])
        for turn in range(WARM_TURNS):
            nc.tensor.matmul(unread[:], zero_block, zero_block, start=True, stop=True)

        ones = held.tile([P, BLOCK], F32, name="ones", align_bytes=64)
        column_number = held.tile([P, BLOCK], F32, name="column_number", align_bytes=64)
        row_number = held.tile([P, BLOCK], F32, name="row_number", align_bytes=64)
        identity = held.tile([P, P], BF16, name="identity")
        nc.vector.memset(ones[:], 1.0)
        nc.vector.tensor_tensor_scan(column_number[:], ones[:], ones[:], 0.0, ALU.mult, ALU.add)
        nc.vector.transpose(row_number[:], column_number[:])
        nc.vector.memset(identity[:], 0.0)
        for q in range(P // BLOCK):
            rows = slice(q * BLOCK, (q + 1) * BLOCK)
            nc.vector.tensor_scalar(
                out=identity[rows, rows],
                in0=column_number[rows, :],
                scalar1=row_number[rows, 0:1],
                scalar2=None,
                op0=ALU.is_equal,
            )
        nc.vector.transpose(bias_columns[:], bias_rows[:])

        window = psum.tile([P, TOKENS], F32, name="window")
        nc.tensor.matmul(window[:], identity[:], base_tile[:], start=True, stop=False)

        piece_columns = PIECE // PER_COLUMN
        cut_pair = list(range(CUT_EXPERTS))
        whole_pair = list(range(CUT_EXPERTS, EXPERTS))
        steps = [(0, cut_pair), (0, whole_pair), (1, whole_pair), (1, cut_pair)]
        for h, pair in steps:
            for kb in range(HALF_BLOCKS):
                for e in pair:
                    if e >= CUT_EXPERTS:
                        weights = w_whole[e - CUT_EXPERTS][:, h * HALF_BLOCKS + kb, :]
                    elif h == 0:
                        weights = w_first[e][:, kb, :]
                    else:
                        weights = w_second[:, e, kb, :]
                    nc.tensor.matmul(
                        window[:].indirect(offsets[:, e * piece_columns : (e + 1) * piece_columns]),
                        weights,
                        x_halves[h][:, kb, e * PIECE : (e + 1) * PIECE],
                        start=False,
                        stop=((h, pair) == steps[-1] and kb == HALF_BLOCKS - 1 and e == pair[-1]),
                    )

        result = held.tile([P, TOKENS], F32, name="result", align_bytes=BURST)
        nc.scalar.activation(result[:], window[:], GELU, bias=bias_columns[:, 0:1])
        nc.sync.dma_start(out, result[:])
